import numpy as np
import ml_dtypes


def mxq(x, axis, fmt="e4m3"):
    dtype, down = {"e4m3": (ml_dtypes.float8_e4m3fn, 7), "e5m2": (ml_dtypes.float8_e5m2, 14)}[fmt]
    v = np.moveaxis(np.asarray(x, np.float32).astype(ml_dtypes.bfloat16).astype(np.float64), axis, -1)
    blocks = v.reshape(v.shape[:-1] + (-1, 32))
    amax = np.abs(blocks).max(-1, keepdims=True)
    byte = np.maximum(np.where(amax > 0, np.frexp(amax)[1] - 1 + 127, 0) - down, 1)
    scale = np.exp2(byte - 127.0)
    codes = (blocks / scale).astype(np.float32).astype(dtype).astype(np.float64)
    return np.moveaxis((codes * scale).reshape(v.shape), -1, axis)


WIDE = False


def mx_kscale(k):
    if not WIDE:
        return np.ones(k)
    levels = np.array([10, -10, 5, -5, 0])
    if k % 512:
        return np.exp2(np.random.permutation(np.resize(levels, k // 32))).repeat(32)
    a = np.empty((k // 512, 16))
    for p in range(k // 512):
        a[p, :8] = np.random.permutation(np.resize(levels, 8))
        for g in range(8):
            far = levels[np.abs(levels - a[p, g]) >= 10]
            a[p, g + 8] = far[np.random.randint(len(far))]
    return np.exp2(a.ravel()).repeat(32)


def f64(x):
    return np.asarray(x).astype(np.float64)


def striped(idx):
    return np.tile(idx.reshape(-1, 16).T, (8, 1)).astype(np.uint16)


def unstriped(offs):
    return offs[:16].T.reshape(-1).astype(np.int64)


def pack_weight(w):
    k, n = w.shape
    w = f64(np.asarray(w, np.float32).astype(ml_dtypes.bfloat16)).reshape(k // 32, 32, n)
    amax = np.abs(w).max(1)
    byte = np.clip(np.where(amax > 0, np.frexp(amax)[1] - 1 + 127 - 7, 1), 1, 254)
    scaled = (w * np.exp2(127.0 - byte)[:, None, :]).reshape(k, n).astype(np.float32)
    words = np.ascontiguousarray(scaled.reshape(k // 512, 128, 4, n).transpose(0, 1, 3, 2)).astype(ml_dtypes.float8_e4m3fn).view(np.uint8)
    return words, np.ascontiguousarray(byte.astype(np.uint8).reshape(k // 512, 16, n))


def unpack_weight(words, scales):
    g, p, n, _ = words.shape
    vals = np.ascontiguousarray(words).view(ml_dtypes.float8_e4m3fn).astype(np.float64) * np.repeat(np.exp2(scales.astype(np.float64) - 127.0), 8, axis=1)[..., None]
    return vals.transpose(0, 1, 3, 2).reshape(g * 512, n)


E2M1 = np.array([0.0, 0.5, 1.0, 1.5, 2.0, 3.0, 4.0, 6.0, -0.0, -0.5, -1.0, -1.5, -2.0, -3.0, -4.0, -6.0])


def pack_fp4(w):
    k, n = w.shape
    w = f64(np.asarray(w, np.float32).astype(ml_dtypes.bfloat16)).reshape(k // 32, 32, n)
    amax = np.abs(w).max(1)
    mant, ex = np.frexp(amax / 6.0)
    byte = np.clip(np.where(amax > 0, np.where(mant > 0.5, ex, ex - 1) + 127, 1), 1, 254)
    scaled = (w * np.exp2(127.0 - byte)[:, None, :]).reshape(k, n).astype(np.float32)
    c = np.ascontiguousarray(scaled.reshape(k // 512, 128, 4, n).transpose(0, 1, 3, 2)).astype(ml_dtypes.float4_e2m1fn).view(np.uint8) & 0xF
    words = (c[..., 0::2] | (c[..., 1::2] << 4)).reshape(k // 512, 128, 2 * n)
    return np.ascontiguousarray(words), np.ascontiguousarray(byte.astype(np.uint8).reshape(k // 512, 16, n))


def unpack_fp4(words, scales):
    g, _, n = scales.shape
    words = np.ascontiguousarray(words).reshape(g, 128, n, 2)
    nib = np.empty((g, 128, n, 4), np.uint8)
    nib[..., 0::2] = words & 0xF
    nib[..., 1::2] = words >> 4
    vals = E2M1[nib] * np.repeat(np.exp2(scales.astype(np.float64) - 127.0), 8, axis=1)[..., None]
    return vals.transpose(0, 1, 3, 2).reshape(g * 512, n)


K, T, S, N, H = 1024, 2048, 512, 256, 512


def setup_inputs():
    n = np.random.standard_normal
    s = mx_kscale(K)[:, None]
    u = mx_kscale(H)
    packed_xT = pack_weight(n((K, T)) * s)
    packed_w1 = pack_fp4(n((K, H)) / np.sqrt(K) / s)
    packed_w2 = pack_fp4(n((K, H)) / np.sqrt(K) / s)
    packed_w3 = pack_fp4(n((H, N)) / np.sqrt(H) / u[:, None])
    return {
        "x_words": packed_xT[0],
        "x_scales": packed_xT[1],
        "w1_words": packed_w1[0],
        "w1_scales": packed_w1[1],
        "w2_words": packed_w2[0],
        "w2_scales": packed_w2[1],
        "ell": (0.4 * n((H, S))).astype(np.float32),
        "flx": (np.random.uniform(0.5, 1.5, (H, S))).astype(np.float32),
        "unit": (np.random.uniform(0.6, 1.4, (H, 1)) * u[:, None]).astype(np.float32),
        "w3_words": packed_w3[0],
        "w3_scales": packed_w3[1],
        "offs": striped(np.random.permutation(T)[:S]),
        "src": striped(np.random.permutation(S)),
    }


def reference(x_words, x_scales, w1_words, w1_scales, w2_words, w2_scales, ell, flx, unit, w3_words, w3_scales, offs, src):
    xq = unpack_weight(x_words, x_scales)[:, unstriped(offs)]
    sh = unpack_fp4(w2_words, w2_scales).T @ xq
    shear = 0.3 * np.tanh(sh)
    kp = unpack_fp4(w1_words, w1_scales).T @ xq
    kappa = 0.4 * np.tanh(kp)
    red = shear / (-1.0 * kappa + 1.0)
    obs = (f64(ell) + red) / (red * f64(ell)[:, unstriped(src)] + 1.0)
    magn = f64(flx) / ((-1.0 * kappa + 1.0) ** 2 - ((shear) ** 2) + 0.2)
    rs = red[:, unstriped(src)]
    hid = f64(unit) * (obs - ((0.5 * np.log(magn)) * rs))
    return unpack_fp4(w3_words, w3_scales).T @ mxq(hid, 0, "e4m3")

@@ -1,0 +1,217 @@
+import math
+from contextlib import ExitStack
+
+import concourse.mybir as mybir
+
+K, T, S, N, H = 1024, 2048, 512, 256, 512
+FLOPS = 2 * (2 * K * H * S + H * N * S)
+
+F32 = mybir.dt.float32
+BF16 = mybir.dt.bfloat16
+I32 = mybir.dt.int32
+U32 = mybir.dt.uint32
+U16 = mybir.dt.uint16
+U8 = mybir.dt.uint8
+FP8X4 = mybir.dt.float8_e4m3fn_x4
+FP4X4 = mybir.dt.float4_e2m1fn_x4
+ALU = mybir.AluOpType
+ACT = mybir.ActivationFunctionType
+
+P = 128
+PACK = 4
+PASSES = K // (P * PACK)
+QUADS = 4
+HALVES = 2
+HALF = S // HALVES
+LIST_COLS = S // 16
+
+
+def tile_picked_ylensg_log_p_kernel(
+    tc, x_words, x_scales, w1_words, w1_scales, w2_words, w2_scales, ell, flx, unit, w3_words, w3_scales, offs, src, out
+):
+    nc = tc.nc
+    with ExitStack() as ctx:
+        held = ctx.enter_context(tc.tile_pool(name="held", bufs=1))
+        psum = ctx.enter_context(tc.psum_pool(name="psum", bufs=1))
+
+        def quad(q):
+            return slice(32 * q, 32 * q + 4)
+
+        def rows(q):
+            return slice(4 * q, 4 * q + 4)
+
+        offs_t = held.tile([P, LIST_COLS], U16, name="offs_t")
+        src_t = held.tile([P, LIST_COLS], U16, name="src_t")
+        xw = [held.tile([P, T], I32, name="xw%d" % o, align_bytes=64) for o in range(PASSES)]
+        xs = held.tile([P, PASSES, T], U8, name="xs", align_bytes=64)
+        w_raw = [held.tile([P, PASSES, 2 * H], U8, name="w_raw%d" % i, align_bytes=64) for i in range(2)]
+        ws_raw = [held.tile([P, PASSES, H], U8, name="ws_raw%d" % i, align_bytes=64) for i in range(2)]
+        w3w = held.tile([P, 2 * N], U8, name="w3w", align_bytes=64)
+        w3s = held.tile([P, N], U8, name="w3s", align_bytes=64)
+        ell_t = [held.tile([P, S], F32, name="ell_t%d" % t) for t in range(PACK)]
+        flx_t = held.tile([P, PACK, S], F32, name="flx_t")
+        unit_t = held.tile([P, PACK], F32, name="unit_t")
+
+        nc.vector.memset(xs[:].bitcast(I32), 0)
+        for i in range(2):
+            nc.gpsimd.memset(ws_raw[i][:].bitcast(I32), 0)
+        nc.gpsimd.memset(w3s[:].bitcast(I32), 0)
+
+        def load_x_words(o):
+            nc.sync.dma_start(xw[o][:], x_words[o].rearrange("p n r -> p (n r)").bitcast(I32))
+
+        nc.sync.dma_start(offs_t[:], offs)
+        load_x_words(0)
+        for q in range(QUADS):
+            nc.sync.dma_start(
+                xs[quad(q), :, :].bitcast(I32), x_scales[:, rows(q), :].rearrange("o r c -> r o c").bitcast(I32)
+            )
+        for i, words in enumerate((w1_words, w2_words)):
+            nc.sync.dma_start(w_raw[i][:].bitcast(I32), words.rearrange("o p c -> p o c").bitcast(I32))
+        load_x_words(1)
+        nc.sync.dma_start(src_t[:], src)
+
+        def load_w_scales(engine, i, scales):
+            for q in range(QUADS):
+                engine.dma_start(
+                    ws_raw[i][quad(q), :, :].bitcast(I32),
+                    scales[:, rows(q), :].rearrange("o r c -> r o c").bitcast(I32),
+                )
+
+        load_w_scales(nc.gpsimd, 0, w1_scales)
+        load_w_scales(nc.sync, 1, w2_scales)
+        ell_v = ell.rearrange("(p t) j -> p t j", t=PACK)
+        for t in range(PACK):
+            nc.sync.dma_start(ell_t[t][:], ell_v[:, t, :])
+        nc.sync.dma_start(flx_t[:], flx.rearrange("(p t) j -> p t j", t=PACK))
+        nc.sync.dma_start(unit_t[:], unit.rearrange("(p t) o -> p (t o)", t=PACK))
+        nc.sync.dma_start(w3w[:].bitcast(I32), w3_words[0].bitcast(I32))
+        for q in range(QUADS):
+            nc.sync.dma_start(w3s[quad(q), :].bitcast(I32), w3_scales[0, rows(q), :].bitcast(I32))
+
+        gw = [held.tile([P, S], U32, name="gw%d" % o, align_bytes=64) for o in range(PASSES)]
+        gs = [held.tile([P, S], U8, name="gs%d" % o, align_bytes=64) for o in range(PASSES)]
+        w_dealt = [held.tile([P, PASSES, PACK, 2 * P], U8, name="w_dealt%d" % i, align_bytes=64) for i in range(2)]
+        ws_dealt = [held.tile([P, PASSES, PACK, P], U8, name="ws_dealt%d" % i, align_bytes=64) for i in range(2)]
+
+        for o in range(PASSES):
+            nc.vector.tensor_copy(gs[o][:], xs[:, o, :].indirect(offs_t[:]))
+        nc.vector.tensor_copy(gw[0][:], xw[0][:].bitcast(U32).indirect(offs_t[:]))
+        for i in range(2):
+            nc.vector.tensor_copy(
+                w_dealt[i][:].rearrange("p o t (m b) -> p o t m b", b=2),
+                w_raw[i][:].rearrange("p o (m t b) -> p o t m b", t=PACK, b=2),
+            )
+            nc.vector.tensor_copy(ws_dealt[i][:], ws_raw[i][:].rearrange("p o (m t) -> p o t m", t=PACK))
+        nc.vector.tensor_copy(gw[1][:], xw[1][:].bitcast(U32).indirect(offs_t[:]))
+
+        u14 = held.tile([P, PACK], F32, name="u14")
+        nc.vector.tensor_scalar(u14[:], unit_t[:], 1.0 / 14.0, None, ALU.mult)
+
+        banks = [[psum.tile([P, S], F32, name="bank%d_%d" % (i, t)) for t in range(PACK)] for i in range(2)]
+        for o in range(PASSES):
+            for t in range(PACK):
+                for i in range(2):
+                    nc.tensor.matmul_mx(
+                        out=banks[i][t][:],
+                        lhsT=w_dealt[i][:, o, t, :].bitcast(FP4X4),
+                        lhsT_scale=ws_dealt[i][:, o, t, :],
+                        rhs=gw[o][:].bitcast(FP8X4),
+                        rhs_scale=gs[o][:],
+                        start=(o == 0),
+                        stop=(o == PASSES - 1),
+                    )
+
+        def plane(name):
+            return held.tile([P, PACK, S], F32, name=name)
+
+        shifted = plane("shifted")
+        t1 = plane("t1")
+        t2 = plane("t2")
+        d_sq = plane("d_sq")
+        shear_sq = plane("shear_sq")
+        q_part = plane("q_part")
+        den = plane("den")
+        num = plane("num")
+        red7 = [held.tile([P, S], F32, name="red7_%d" % t) for t in range(PACK)]
+
+        def cols(h):
+            return slice(h * HALF, (h + 1) * HALF)
+
+        def entries(h):
+            return src_t[:, h * LIST_COLS // HALVES : (h + 1) * LIST_COLS // HALVES]
+
+        for t in range(PACK):
+            nc.scalar.activation(shifted[:, t, :], banks[0][t][:], ACT.Tanh, bias=0.5 * math.log(3.0 / 7.0))
+            nc.scalar.activation(t2[:, t, :], banks[1][t][:], ACT.Tanh)
+            nc.scalar.activation(t1[:, t, :], banks[0][t][:], ACT.Tanh)
+            nc.scalar.activation(shear_sq[:, t, :], t2[:, t, :], ACT.Square, scale=0.3)
+            nc.scalar.activation(d_sq[:, t, :], t1[:, t, :], ACT.Square, scale=-0.4, bias=1.0)
+            nc.vector.scalar_tensor_tensor(red7[t][:], shifted[:, t, :], 2.5, t2[:, t, :], ALU.add, ALU.mult)
+            for h in range(HALVES):
+                nc.vector.tensor_tensor(
+                    den[:, t, cols(h)], ell_t[t][:].indirect(entries(h)), red7[t][:, cols(h)], ALU.mult
+                )
+            nc.vector.tensor_tensor(q_part[:, t, :], d_sq[:, t, :], shear_sq[:, t, :], ALU.subtract)
+
+        for t in range(PACK):
+            nc.vector.scalar_tensor_tensor(num[:, t, :], ell_t[t][:], 7.0, red7[t][:], ALU.mult, ALU.add)
+        half_sign = plane("half_sign")
+        nc.vector.tensor_scalar(half_sign[:], den[:], -7.0, 0.5, ALU.is_ge, ALU.subtract)
+
+        ln_flx = t1
+        ln_q = plane("ln_q")
+        ln_ratio = plane("ln_ratio")
+        pulled = plane("pulled")
+        for h in range(HALVES):
+            nc.scalar.activation(ln_flx[:, :, cols(h)], flx_t[:, :, cols(h)], ACT.Ln)
+            nc.scalar.activation(ln_q[:, :, cols(h)], q_part[:, :, cols(h)], ACT.Ln, bias=0.2)
+            nc.vector.tensor_tensor(ln_ratio[:, :, cols(h)], ln_q[:, :, cols(h)], ln_flx[:, :, cols(h)], ALU.subtract)
+            for t in range(PACK):
+                nc.vector.tensor_tensor(
+                    pulled[:, t, cols(h)], red7[t][:].indirect(entries(h)), ln_ratio[:, t, cols(h)], ALU.mult
+                )
+
+        signed_num = plane("signed_num")
+        for t in range(PACK):
+            nc.vector.scalar_tensor_tensor(
+                signed_num[:, t, :], num[:, t, :], u14[:, t : t + 1], half_sign[:, t, :], ALU.mult, ALU.mult
+            )
+
+        inv_root = q_part
+        inv_abs = plane("inv_abs")
+        obs = plane("obs")
+        hid = held.tile([P, PACK, S], BF16, name="hid")
+        out_v = out.rearrange("(g p) j -> p g j", p=P)
+        for h in range(HALVES):
+            nc.scalar.activation(
+                inv_root[:, :, cols(h)], den[:, :, cols(h)], ACT.Abs_reciprocal_sqrt, scale=1.0 / 7.0, bias=1.0
+            )
+            nc.scalar.activation(inv_abs[:, :, cols(h)], inv_root[:, :, cols(h)], ACT.Square, scale=2.0)
+        for h in range(HALVES):
+            nc.vector.tensor_tensor(obs[:, :, cols(h)], signed_num[:, :, cols(h)], inv_abs[:, :, cols(h)], ALU.mult)
+            for t in range(PACK):
+                nc.vector.scalar_tensor_tensor(
+                    hid[:, t, cols(h)], pulled[:, t, cols(h)], u14[:, t : t + 1], obs[:, t, cols(h)], ALU.mult, ALU.add
+                )
+            woven = held.tile([P, HALF, PACK], BF16, name="woven%d" % h, align_bytes=64)
+            nc.scalar.copy(woven[:], hid[:, :, cols(h)].rearrange("p t j -> p j t"))
+            codes = held.tile([P, HALF], U32, name="codes%d" % h, align_bytes=64)
+            code_scales = held.tile([P, HALF], U8, name="code_scales%d" % h, align_bytes=64)
+            nc.vector.quantize_mx(
+                out=codes[:].bitcast(FP8X4), scales=code_scales[:], in_=woven[:].rearrange("p j t -> p (j t)")
+            )
+            acc = banks[h][0]
+            for g in range(N // P):
+                nc.tensor.matmul_mx(
+                    out=acc[:, g * HALF : (g + 1) * HALF],
+                    lhsT=w3w[:, 2 * P * g : 2 * P * (g + 1)].bitcast(FP4X4),
+                    lhsT_scale=w3s[:, P * g : P * (g + 1)],
+                    rhs=codes[:].bitcast(FP8X4),
+                    rhs_scale=code_scales[:],
+                    start=True,
+                    stop=True,
+                )
+            result = held.tile([P, N // P, HALF], F32, name="result%d" % h)
+            nc.scalar.copy(result[:], acc[:].rearrange("p (g j) -> p g j", g=N // P))
+            nc.sync.dma_start(out_v[:, :, cols(h)], result[:])

@@ -2,6 +2,7 @@ import math
 from contextlib import ExitStack
 
 import concourse.mybir as mybir
+from concourse.masks import make_identity
 
 K, T, S, N, H = 1024, 2048, 512, 256, 512
 FLOPS = 2 * (2 * K * H * S + H * N * S)
@@ -21,6 +22,7 @@ P = 128
 PACK = 4
 PASSES = K // (P * PACK)
 QUADS = 4
+BLOCKS = S // P
 HALVES = 2
 HALF = S // HALVES
 LIST_COLS = S // 16
@@ -34,184 +36,220 @@ def tile_picked_ylensg_log_p_kernel(
         held = ctx.enter_context(tc.tile_pool(name="held", bufs=1))
         psum = ctx.enter_context(tc.psum_pool(name="psum", bufs=1))
 
+        def sbuf(shape, dtype, name, slot=None):
+            return held.tile(shape, dtype, name=name, tag=slot or name, align_bytes=64)
+
+        def bank(shape, name, slot):
+            return psum.tile(shape, F32, name=name, tag=slot)
+
         def quad(q):
             return slice(32 * q, 32 * q + 4)
 
         def rows(q):
             return slice(4 * q, 4 * q + 4)
 
-        offs_t = held.tile([P, LIST_COLS], U16, name="offs_t")
-        src_t = held.tile([P, LIST_COLS], U16, name="src_t")
-        xw = [held.tile([P, T], I32, name="xw%d" % o, align_bytes=64) for o in range(PASSES)]
-        xs = held.tile([P, PASSES, T], U8, name="xs", align_bytes=64)
-        w_raw = [held.tile([P, PASSES, 2 * H], U8, name="w_raw%d" % i, align_bytes=64) for i in range(2)]
-        ws_raw = [held.tile([P, PASSES, H], U8, name="ws_raw%d" % i, align_bytes=64) for i in range(2)]
-        w3w = held.tile([P, 2 * N], U8, name="w3w", align_bytes=64)
-        w3s = held.tile([P, N], U8, name="w3s", align_bytes=64)
-        ell_t = [held.tile([P, S], F32, name="ell_t%d" % t) for t in range(PACK)]
-        flx_t = held.tile([P, PACK, S], F32, name="flx_t")
-        unit_t = held.tile([P, PACK], F32, name="unit_t")
-
-        nc.vector.memset(xs[:].bitcast(I32), 0)
-        for i in range(2):
-            nc.gpsimd.memset(ws_raw[i][:].bitcast(I32), 0)
-        nc.gpsimd.memset(w3s[:].bitcast(I32), 0)
-
-        def load_x_words(o):
-            nc.sync.dma_start(xw[o][:], x_words[o].rearrange("p n r -> p (n r)").bitcast(I32))
-
-        nc.sync.dma_start(offs_t[:], offs)
-        load_x_words(0)
-        for q in range(QUADS):
-            nc.sync.dma_start(
-                xs[quad(q), :, :].bitcast(I32), x_scales[:, rows(q), :].rearrange("o r c -> r o c").bitcast(I32)
-            )
-        for i, words in enumerate((w1_words, w2_words)):
-            nc.sync.dma_start(w_raw[i][:].bitcast(I32), words.rearrange("o p c -> p o c").bitcast(I32))
-        load_x_words(1)
-        nc.sync.dma_start(src_t[:], src)
-
-        def load_w_scales(engine, i, scales):
-            for q in range(QUADS):
-                engine.dma_start(
-                    ws_raw[i][quad(q), :, :].bitcast(I32),
-                    scales[:, rows(q), :].rearrange("o r c -> r o c").bitcast(I32),
-                )
-
-        load_w_scales(nc.gpsimd, 0, w1_scales)
-        load_w_scales(nc.sync, 1, w2_scales)
-        ell_v = ell.rearrange("(p t) j -> p t j", t=PACK)
-        for t in range(PACK):
-            nc.sync.dma_start(ell_t[t][:], ell_v[:, t, :])
-        nc.sync.dma_start(flx_t[:], flx.rearrange("(p t) j -> p t j", t=PACK))
-        nc.sync.dma_start(unit_t[:], unit.rearrange("(p t) o -> p (t o)", t=PACK))
-        nc.sync.dma_start(w3w[:].bitcast(I32), w3_words[0].bitcast(I32))
-        for q in range(QUADS):
-            nc.sync.dma_start(w3s[quad(q), :].bitcast(I32), w3_scales[0, rows(q), :].bitcast(I32))
-
-        gw = [held.tile([P, S], U32, name="gw%d" % o, align_bytes=64) for o in range(PASSES)]
-        gs = [held.tile([P, S], U8, name="gs%d" % o, align_bytes=64) for o in range(PASSES)]
-        w_dealt = [held.tile([P, PASSES, PACK, 2 * P], U8, name="w_dealt%d" % i, align_bytes=64) for i in range(2)]
-        ws_dealt = [held.tile([P, PASSES, PACK, P], U8, name="ws_dealt%d" % i, align_bytes=64) for i in range(2)]
-
-        for o in range(PASSES):
-            nc.vector.tensor_copy(gs[o][:], xs[:, o, :].indirect(offs_t[:]))
-        nc.vector.tensor_copy(gw[0][:], xw[0][:].bitcast(U32).indirect(offs_t[:]))
-        for i in range(2):
-            nc.vector.tensor_copy(
-                w_dealt[i][:].rearrange("p o t (m b) -> p o t m b", b=2),
-                w_raw[i][:].rearrange("p o (m t b) -> p o t m b", t=PACK, b=2),
-            )
-            nc.vector.tensor_copy(ws_dealt[i][:], ws_raw[i][:].rearrange("p o (m t) -> p o t m", t=PACK))
-        nc.vector.tensor_copy(gw[1][:], xw[1][:].bitcast(U32).indirect(offs_t[:]))
-
-        u14 = held.tile([P, PACK], F32, name="u14")
-        nc.vector.tensor_scalar(u14[:], unit_t[:], 1.0 / 14.0, None, ALU.mult)
-
-        banks = [[psum.tile([P, S], F32, name="bank%d_%d" % (i, t)) for t in range(PACK)] for i in range(2)]
-        for o in range(PASSES):
-            for t in range(PACK):
-                for i in range(2):
-                    nc.tensor.matmul_mx(
-                        out=banks[i][t][:],
-                        lhsT=w_dealt[i][:, o, t, :].bitcast(FP4X4),
-                        lhsT_scale=ws_dealt[i][:, o, t, :],
-                        rhs=gw[o][:].bitcast(FP8X4),
-                        rhs_scale=gs[o][:],
-                        start=(o == 0),
-                        stop=(o == PASSES - 1),
-                    )
-
-        def plane(name):
-            return held.tile([P, PACK, S], F32, name=name)
-
-        shifted = plane("shifted")
-        t1 = plane("t1")
-        t2 = plane("t2")
-        d_sq = plane("d_sq")
-        shear_sq = plane("shear_sq")
-        q_part = plane("q_part")
-        den = plane("den")
-        num = plane("num")
-        red7 = [held.tile([P, S], F32, name="red7_%d" % t) for t in range(PACK)]
-
         def cols(h):
             return slice(h * HALF, (h + 1) * HALF)
 
-        def entries(h):
-            return src_t[:, h * LIST_COLS // HALVES : (h + 1) * LIST_COLS // HALVES]
+        def block(b):
+            return slice(b * P, (b + 1) * P)
 
-        for t in range(PACK):
-            nc.scalar.activation(shifted[:, t, :], banks[0][t][:], ACT.Tanh, bias=0.5 * math.log(3.0 / 7.0))
-            nc.scalar.activation(t2[:, t, :], banks[1][t][:], ACT.Tanh)
-            nc.scalar.activation(t1[:, t, :], banks[0][t][:], ACT.Tanh)
-            nc.scalar.activation(shear_sq[:, t, :], t2[:, t, :], ACT.Square, scale=0.3)
-            nc.scalar.activation(d_sq[:, t, :], t1[:, t, :], ACT.Square, scale=-0.4, bias=1.0)
-            nc.vector.scalar_tensor_tensor(red7[t][:], shifted[:, t, :], 2.5, t2[:, t, :], ALU.add, ALU.mult)
+        def list_half(entries, h):
+            return entries[:, h * LIST_COLS // HALVES : (h + 1) * LIST_COLS // HALVES]
+
+        offs_t = held.tile([P, LIST_COLS], U16, name="offs_t")
+        src_t = held.tile([P, LIST_COLS], U16, name="src_t")
+        xw = [sbuf([P, T], I32, "xw%d" % o) for o in range(PASSES)]
+        xs = sbuf([P, PASSES, T], U8, "xs")
+        w1w = sbuf([P, PASSES, 2 * H], U8, "w1w")
+        w2w = sbuf([P, PASSES, 2 * H], U8, "w2w")
+        w1s = sbuf([P, PASSES, H], U8, "w1s")
+        w2s = sbuf([P, PASSES, H], U8, "w2s")
+
+        nc.vector.memset(xs[:].bitcast(I32), 0)
+        nc.gpsimd.memset(w2s[:].bitcast(I32), 0)
+        nc.gpsimd.memset(w1s[:].bitcast(I32), 0)
+
+        def load_scale_rows(engine, plane, scales):
+            for q in range(QUADS):
+                engine.dma_start(
+                    plane[quad(q), :, :].bitcast(I32), scales[:, rows(q), :].rearrange("o r c -> r o c").bitcast(I32)
+                )
+
+        nc.sync.dma_start(offs_t[:], offs)
+        nc.sync.dma_start(src_t[:], src)
+        for o in range(PASSES):
+            nc.sync.dma_start(xw[o][:], x_words[o].rearrange("p n r -> p (n r)").bitcast(I32))
+        nc.sync.dma_start(w2w[:].bitcast(I32), w2_words.rearrange("o p c -> p o c").bitcast(I32))
+        nc.sync.dma_start(w1w[:].bitcast(I32), w1_words.rearrange("o p c -> p o c").bitcast(I32))
+        load_scale_rows(nc.sync, xs, x_scales)
+        load_scale_rows(nc.gpsimd, w2s, w2_scales)
+        load_scale_rows(nc.gpsimd, w1s, w1_scales)
+
+        ident = sbuf([P, P], F32, "ident")
+        make_identity(nc, ident[:])
+
+        gw = [sbuf([P, S], U32, "gw%d" % o) for o in range(PASSES)]
+        gs = [sbuf([P, S], U8, "gs%d" % o) for o in range(PASSES)]
+        nc.vector.tensor_copy(gw[0][:], xw[0][:].bitcast(U32).indirect(offs_t[:]))
+        for o in range(PASSES):
+            nc.vector.tensor_copy(gs[o][:], xs[:, o, :].indirect(offs_t[:]))
+        for h in range(HALVES):
+            nc.vector.tensor_copy(gw[1][:, cols(h)], xw[1][:].bitcast(U32).indirect(list_half(offs_t, h)))
+
+        ell_t = sbuf([P, PACK, S], F32, "ell_t", "xw0")
+        nc.sync.dma_start(ell_t[:], ell.rearrange("(p t) j -> p t j", t=PACK))
+        unit_t = sbuf([P, PACK], F32, "unit_t", "xs")
+        nc.sync.dma_start(unit_t[:], unit.rearrange("(p t) o -> p (t o)", t=PACK))
+        flx_t = sbuf([P, PACK, S], F32, "flx_t", "xw1")
+        nc.sync.dma_start(flx_t[:], flx.rearrange("(p t) j -> p t j", t=PACK))
+        u14 = sbuf([P, PACK], F32, "u14")
+        nc.gpsimd.tensor_scalar(u14[:], unit_t[:], 1.0 / 14.0, 0.0, ALU.mult, ALU.add)
+
+        def product(name, slot, words, scales, b):
+            acc = bank([P, H], name, slot)
+            for o in range(PASSES):
+                nc.tensor.matmul_mx(
+                    out=acc[:],
+                    lhsT=gw[o][:, block(b)].bitcast(FP8X4),
+                    lhsT_scale=gs[o][:, block(b)],
+                    rhs=words[:, o, :].bitcast(FP4X4),
+                    rhs_scale=scales[:, o, :],
+                    start=(o == 0),
+                    stop=(o == PASSES - 1),
+                )
+            return acc[:].rearrange("p (m t) -> p t m", t=PACK)
+
+        ring = ("ring0", "ring1", "ring2")
+        red_bank = [bank([P, S], "red_bank%d" % t, "red%d" % t) for t in range(PACK)]
+        q_slot = ("spare", ring[2], ring[0], ring[1])
+        ell_src = []
+        d_sqs = []
+        neg_sqs = []
+
+        def cross_q(b):
+            q_bank = bank([P, PACK, P], "q_bank%d" % b, q_slot[b])
+            for t in range(PACK):
+                nc.tensor.matmul(q_bank[:, t, :], d_sqs[b][:, t, :], ident[:], start=True, stop=False, is_transpose=True)
+                nc.tensor.matmul(q_bank[:, t, :], neg_sqs[b][:, t, :], ident[:], start=False, stop=True, is_transpose=True)
+            return q_bank
+
+        q_banks = []
+        for b in range(BLOCKS):
+            sh = product("sh%d" % b, ring[(2 * b) % 3], w2w, w2s, b)
+            t2 = sbuf([P, PACK, P], F32, "t2_%d" % b)
+            nc.scalar.activation(t2[:], sh, ACT.Tanh)
+            kp = product("kp%d" % b, ring[(2 * b + 1) % 3], w1w, w1s, b)
+            shifted = sbuf([P, PACK, P], F32, "shifted%d" % b)
+            t1 = sbuf([P, PACK, P], F32, "t1_%d" % b)
+            nc.scalar.activation(shifted[:], kp, ACT.Tanh, bias=0.5 * math.log(3.0 / 7.0))
+            nc.scalar.activation(t1[:], kp, ACT.Tanh)
+            d_sq = sbuf([P, PACK, P], F32, "d_sq%d" % b)
+            nc.scalar.activation(d_sq[:], t1[:], ACT.Square, scale=-0.4, bias=1.0)
+            red7 = sbuf([P, PACK, P], F32, "red7_%d" % b)
+            neg_sq = sbuf([P, PACK, P], F32, "neg_sq%d" % b)
+            nc.vector.scalar_tensor_tensor(neg_sq[:], t2[:], -0.09, t2[:], ALU.mult, ALU.mult)
+            nc.vector.scalar_tensor_tensor(red7[:], shifted[:], 2.5, t2[:], ALU.add, ALU.mult)
+            for t in range(PACK):
+                nc.tensor.transpose(red_bank[t][:, block(b)], red7[:, t, :], ident[:])
+            d_sqs.append(d_sq)
+            neg_sqs.append(neg_sq)
+            if b == 0:
+                q_banks.append(cross_q(0))
+            picked = sbuf([P, S], F32, "ell_src%d" % b, "shifted%d" % b)
             for h in range(HALVES):
-                nc.vector.tensor_tensor(
-                    den[:, t, cols(h)], ell_t[t][:].indirect(entries(h)), red7[t][:, cols(h)], ALU.mult
-                )
-            nc.vector.tensor_tensor(q_part[:, t, :], d_sq[:, t, :], shear_sq[:, t, :], ALU.subtract)
+                nc.vector.tensor_copy(picked[:, cols(h)], ell_t[:, b, :].indirect(list_half(src_t, h)))
+            ell_src.append(picked)
+        for b in range(1, BLOCKS):
+            q_banks.append(cross_q(b))
 
+        w3w = sbuf([P, 2 * N], U8, "w3w", "w2w")
+        nc.sync.dma_start(w3w[:].bitcast(I32), w3_words[0].bitcast(I32))
+        w3s = sbuf([P, 1, N], U8, "w3s", "w2s")
+        nc.gpsimd.memset(w3s[:].bitcast(I32), 0)
+        load_scale_rows(nc.sync, w3s, w3_scales)
+
+        den = sbuf([P, PACK, S], F32, "den")
+        num = sbuf([P, PACK, S], F32, "num")
+        window = [sbuf([P, S], F32, "window%d" % t) for t in range(PACK)]
         for t in range(PACK):
-            nc.vector.scalar_tensor_tensor(num[:, t, :], ell_t[t][:], 7.0, red7[t][:], ALU.mult, ALU.add)
-        half_sign = plane("half_sign")
-        nc.vector.tensor_scalar(half_sign[:], den[:], -7.0, 0.5, ALU.is_ge, ALU.subtract)
+            nc.vector.tensor_tensor(den[:, t, :], red_bank[t][:], ell_src[t][:], ALU.mult)
+            nc.vector.scalar_tensor_tensor(num[:, t, :], ell_t[:, t, :], 7.0, red_bank[t][:], ALU.mult, ALU.add)
 
-        ln_flx = t1
-        ln_q = plane("ln_q")
-        ln_ratio = plane("ln_ratio")
-        pulled = plane("pulled")
+        pulled = sbuf([P, PACK, S], F32, "pulled")
+        late_slots = (("t1_3", "d_sq3"), ("t2_3", "ln_q1"))
         for h in range(HALVES):
-            nc.scalar.activation(ln_flx[:, :, cols(h)], flx_t[:, :, cols(h)], ACT.Ln)
-            nc.scalar.activation(ln_q[:, :, cols(h)], q_part[:, :, cols(h)], ACT.Ln, bias=0.2)
-            nc.vector.tensor_tensor(ln_ratio[:, :, cols(h)], ln_q[:, :, cols(h)], ln_flx[:, :, cols(h)], ALU.subtract)
+            ln_flx = sbuf([P, PACK, HALF], F32, "ln_flx%d" % h, late_slots[h][0])
+            ln_q = sbuf([P, PACK, HALF], F32, "ln_q%d" % h, late_slots[h][1])
+            ln_ratio = sbuf([P, PACK, HALF], F32, "ln_ratio%d" % h)
+            nc.scalar.activation(ln_flx[:], flx_t[:, :, cols(h)], ACT.Ln)
+            for c in range(BLOCKS // HALVES):
+                nc.scalar.activation(ln_q[:, :, block(c)], q_banks[2 * h + c][:], ACT.Ln, bias=0.2)
+            if h == 0:
+                for t in range(PACK):
+                    nc.scalar.activation(window[t][:], red_bank[t][:], ACT.Copy, scale=u14[:, t : t + 1])
+            nc.vector.tensor_tensor(ln_ratio[:], ln_q[:], ln_flx[:], ALU.subtract)
             for t in range(PACK):
                 nc.vector.tensor_tensor(
-                    pulled[:, t, cols(h)], red7[t][:].indirect(entries(h)), ln_ratio[:, t, cols(h)], ALU.mult
+                    pulled[:, t, cols(h)], window[t][:].indirect(list_half(src_t, h)), ln_ratio[:, t, :], ALU.mult
                 )
 
-        signed_num = plane("signed_num")
+        sign = sbuf([P, PACK, S], F32, "sign")
+        signed_num = sbuf([P, PACK, S], F32, "signed_num")
         for t in range(PACK):
+            nc.scalar.activation(sign[:, t, :], den[:, t, :], ACT.Sign, scale=1.0 / 7.0, bias=1.0)
             nc.vector.scalar_tensor_tensor(
-                signed_num[:, t, :], num[:, t, :], u14[:, t : t + 1], half_sign[:, t, :], ALU.mult, ALU.mult
+                signed_num[:, t, :], num[:, t, :], u14[:, t : t + 1], sign[:, t, :], ALU.mult, ALU.mult
             )
 
-        inv_root = q_part
-        inv_abs = plane("inv_abs")
-        obs = plane("obs")
-        hid = held.tile([P, PACK, S], BF16, name="hid")
+        inv_root = sbuf([P, PACK, S], F32, "inv_root", "xw1")
+        inv_abs = sbuf([P, PACK, S], F32, "inv_abs")
+        obs = sbuf([P, PACK, S], F32, "obs")
+        hid = sbuf([P, PACK, S], BF16, "hid")
         out_v = out.rearrange("(g p) j -> p g j", p=P)
-        for h in range(HALVES):
+        for c in range(BLOCKS):
             nc.scalar.activation(
-                inv_root[:, :, cols(h)], den[:, :, cols(h)], ACT.Abs_reciprocal_sqrt, scale=1.0 / 7.0, bias=1.0
+                inv_root[:, :, block(c)], den[:, :, block(c)], ACT.Abs_reciprocal_sqrt, scale=1.0 / 14.0, bias=0.5
             )
-            nc.scalar.activation(inv_abs[:, :, cols(h)], inv_root[:, :, cols(h)], ACT.Square, scale=2.0)
-        for h in range(HALVES):
-            nc.vector.tensor_tensor(obs[:, :, cols(h)], signed_num[:, :, cols(h)], inv_abs[:, :, cols(h)], ALU.mult)
-            for t in range(PACK):
-                nc.vector.scalar_tensor_tensor(
-                    hid[:, t, cols(h)], pulled[:, t, cols(h)], u14[:, t : t + 1], obs[:, t, cols(h)], ALU.mult, ALU.add
-                )
-            woven = held.tile([P, HALF, PACK], BF16, name="woven%d" % h, align_bytes=64)
-            nc.scalar.copy(woven[:], hid[:, :, cols(h)].rearrange("p t j -> p j t"))
-            codes = held.tile([P, HALF], U32, name="codes%d" % h, align_bytes=64)
-            code_scales = held.tile([P, HALF], U8, name="code_scales%d" % h, align_bytes=64)
+            nc.scalar.activation(inv_abs[:, :, block(c)], inv_root[:, :, block(c)], ACT.Square)
+
+        def observe(c):
+            nc.vector.tensor_tensor(obs[:, :, block(c)], signed_num[:, :, block(c)], inv_abs[:, :, block(c)], ALU.mult)
+
+        def combine(c):
+            nc.vector.tensor_tensor(hid[:, :, block(c)], pulled[:, :, block(c)], obs[:, :, block(c)], ALU.add)
+
+        def finish(c):
+            woven = sbuf([P, P, PACK], BF16, "woven%d" % c)
+            planes = hid[:, :, block(c)].rearrange("p t j -> p j t")
+            if c < BLOCKS - 1:
+                nc.scalar.copy(woven[:], planes)
+            else:
+                nc.vector.tensor_copy(woven[:], planes)
+            codes = sbuf([P, P], U32, "codes%d" % c)
+            code_scales = sbuf([P, P], U8, "code_scales%d" % c)
             nc.vector.quantize_mx(
                 out=codes[:].bitcast(FP8X4), scales=code_scales[:], in_=woven[:].rearrange("p j t -> p (j t)")
             )
-            acc = banks[h][0]
+            acc = bank([P, N // P, P], "acc%d" % c, "red%d" % c)
             for g in range(N // P):
                 nc.tensor.matmul_mx(
-                    out=acc[:, g * HALF : (g + 1) * HALF],
+                    out=acc[:, g, :],
                     lhsT=w3w[:, 2 * P * g : 2 * P * (g + 1)].bitcast(FP4X4),
-                    lhsT_scale=w3s[:, P * g : P * (g + 1)],
+                    lhsT_scale=w3s[:, 0, block(g)],
                     rhs=codes[:].bitcast(FP8X4),
                     rhs_scale=code_scales[:],
                     start=True,
                     stop=True,
                 )
-            result = held.tile([P, N // P, HALF], F32, name="result%d" % h)
-            nc.scalar.copy(result[:], acc[:].rearrange("p (g j) -> p g j", g=N // P))
-            nc.sync.dma_start(out_v[:, :, cols(h)], result[:])
+            result = sbuf([P, N // P, P], F32, "result%d" % c)
+            nc.scalar.copy(result[:], acc[:])
+            nc.sync.dma_start(out_v[:, :, block(c)], result[:])
+
+        for step in range(BLOCKS + 2):
+            if step < BLOCKS:
+                observe(step)
+            if 1 <= step <= BLOCKS:
+                combine(step - 1)
+            if step >= 2:
+                finish(step - 2)

@@ -66,42 +66,78 @@ def tile_picked_ylensg_log_p_kernel(
         w1s = sbuf([P, PASSES, H], U8, "w1s")
         w2s = sbuf([P, PASSES, H], U8, "w2s")
 
+        ell_t = sbuf([P, PACK, S], F32, "ell_t")
+        ident = sbuf([P, P], F32, "ident")
+        make_identity(nc, ident[:])
         nc.vector.memset(xs[:].bitcast(I32), 0)
-        nc.gpsimd.memset(w2s[:].bitcast(I32), 0)
         nc.gpsimd.memset(w1s[:].bitcast(I32), 0)
+        nc.gpsimd.memset(w2s[:].bitcast(I32), 0)
 
-        def load_scale_rows(engine, plane, scales):
-            for q in range(QUADS):
+        def load_scale_rows(engine, plane, scales, quads):
+            for q in quads:
                 engine.dma_start(
                     plane[quad(q), :, :].bitcast(I32), scales[:, rows(q), :].rearrange("o r c -> r o c").bitcast(I32)
                 )
 
-        nc.sync.dma_start(offs_t[:], offs)
-        nc.sync.dma_start(src_t[:], src)
-        for o in range(PASSES):
+        def load_x_words(o):
             nc.sync.dma_start(xw[o][:], x_words[o].rearrange("p n r -> p (n r)").bitcast(I32))
-        nc.sync.dma_start(w2w[:].bitcast(I32), w2_words.rearrange("o p c -> p o c").bitcast(I32))
-        nc.sync.dma_start(w1w[:].bitcast(I32), w1_words.rearrange("o p c -> p o c").bitcast(I32))
-        load_scale_rows(nc.sync, xs, x_scales)
-        load_scale_rows(nc.gpsimd, w2s, w2_scales)
-        load_scale_rows(nc.gpsimd, w1s, w1_scales)
 
-        ident = sbuf([P, P], F32, "ident")
-        make_identity(nc, ident[:])
+        ell_v = ell.rearrange("(p t) j -> p t j", t=PACK)
+        nc.sync.dma_start(src_t[:], src)
+        for pair in range(2):
+            nc.sync.dma_start(ell_t[:, 2 * pair : 2 * pair + 2, :], ell_v[:, 2 * pair : 2 * pair + 2, :])
+        nc.sync.dma_start(offs_t[:], offs)
+        load_scale_rows(nc.sync, xs, x_scales, range(QUADS))
+        load_x_words(0)
+        load_x_words(1)
+        load_scale_rows(nc.sync, w1s, w1_scales, range(1))
+        load_scale_rows(nc.sync, w2s, w2_scales, range(QUADS))
+        nc.sync.dma_start(w1w[:].bitcast(I32), w1_words.rearrange("o p c -> p o c").bitcast(I32))
+        nc.sync.dma_start(w2w[:].bitcast(I32), w2_words.rearrange("o p c -> p o c").bitcast(I32))
+        load_scale_rows(nc.gpsimd, w1s, w1_scales, range(1, QUADS))
+
+        ell_src = sbuf([P, PACK, S], F32, "ell_src")
+
+        def gather_ell(t):
+            for h in range(HALVES):
+                looked_up = ell_t[:, t, :].indirect(list_half(src_t, h))
+                if t in (0, PACK - 1):
+                    nc.vector.tensor_copy(ell_src[:, t, cols(h)], looked_up)
+                else:
+                    nc.scalar.activation(ell_src[:, t, cols(h)], looked_up, ACT.Copy)
+
+        gather_ell(0)
+        gather_ell(1)
+        ell7 = []
+        for b in range(BLOCKS):
+            turned = bank([P, PACK, P], "ell_bank%d" % b, "red%d" % b)
+            for t in range(PACK):
+                nc.tensor.transpose(turned[:, t, :], ell_t[:, t, block(b)], ident[:])
+            scaled = sbuf([P, PACK, P], F32, "ell7_%d" % b)
+            nc.scalar.activation(scaled[:], turned[:], ACT.Copy, scale=7.0)
+            ell7.append(scaled)
+        gather_ell(2)
 
         gw = [sbuf([P, S], U32, "gw%d" % o) for o in range(PASSES)]
         gs = [sbuf([P, S], U8, "gs%d" % o) for o in range(PASSES)]
-        nc.vector.tensor_copy(gw[0][:], xw[0][:].bitcast(U32).indirect(offs_t[:]))
-        for o in range(PASSES):
-            nc.vector.tensor_copy(gs[o][:], xs[:, o, :].indirect(offs_t[:]))
-        for h in range(HALVES):
-            nc.vector.tensor_copy(gw[1][:, cols(h)], xw[1][:].bitcast(U32).indirect(list_half(offs_t, h)))
 
-        ell_t = sbuf([P, PACK, S], F32, "ell_t", "xw0")
-        nc.sync.dma_start(ell_t[:], ell.rearrange("(p t) j -> p t j", t=PACK))
+        def gather_words(o, h):
+            nc.vector.tensor_copy(gw[o][:, cols(h)], xw[o][:].bitcast(U32).indirect(list_half(offs_t, h)))
+
+        def gather_scales(o, h):
+            nc.vector.tensor_copy(gs[o][:, cols(h)], xs[:, o, :].indirect(list_half(offs_t, h)))
+
+        for h in range(HALVES):
+            for o in range(PASSES):
+                gather_scales(o, h)
+        for o in range(PASSES):
+            for h in range(HALVES):
+                gather_words(o, h)
+
+        gather_ell(3)
         unit_t = sbuf([P, PACK], F32, "unit_t", "xs")
         nc.sync.dma_start(unit_t[:], unit.rearrange("(p t) o -> p (t o)", t=PACK))
-        flx_t = sbuf([P, PACK, S], F32, "flx_t", "xw1")
+        flx_t = sbuf([P, PACK, S], F32, "flx_t", "xw0")
         nc.sync.dma_start(flx_t[:], flx.rearrange("(p t) j -> p t j", t=PACK))
         u14 = sbuf([P, PACK], F32, "u14")
         nc.gpsimd.tensor_scalar(u14[:], unit_t[:], 1.0 / 14.0, 0.0, ALU.mult, ALU.add)
@@ -120,10 +156,10 @@ def tile_picked_ylensg_log_p_kernel(
                 )
             return acc[:].rearrange("p (m t) -> p t m", t=PACK)
 
-        ring = ("ring0", "ring1", "ring2")
+        ring = ("ring0", "ring1", "ring2", "ring3")
         red_bank = [bank([P, S], "red_bank%d" % t, "red%d" % t) for t in range(PACK)]
-        q_slot = ("spare", ring[2], ring[0], ring[1])
-        ell_src = []
+        q_slot = ring
+        red7s = []
         d_sqs = []
         neg_sqs = []
 
@@ -136,46 +172,40 @@ def tile_picked_ylensg_log_p_kernel(
 
         q_banks = []
         for b in range(BLOCKS):
-            sh = product("sh%d" % b, ring[(2 * b) % 3], w2w, w2s, b)
-            t2 = sbuf([P, PACK, P], F32, "t2_%d" % b)
-            nc.scalar.activation(t2[:], sh, ACT.Tanh)
-            kp = product("kp%d" % b, ring[(2 * b + 1) % 3], w1w, w1s, b)
+            kp = product("kp%d" % b, ring[(2 * b) % 4], w1w, w1s, b)
+            sh = product("sh%d" % b, ring[(2 * b + 1) % 4], w2w, w2s, b)
             shifted = sbuf([P, PACK, P], F32, "shifted%d" % b)
             t1 = sbuf([P, PACK, P], F32, "t1_%d" % b)
+            t2 = sbuf([P, PACK, P], F32, "t2_%d" % b)
             nc.scalar.activation(shifted[:], kp, ACT.Tanh, bias=0.5 * math.log(3.0 / 7.0))
+            nc.scalar.activation(t2[:], sh, ACT.Tanh)
             nc.scalar.activation(t1[:], kp, ACT.Tanh)
             d_sq = sbuf([P, PACK, P], F32, "d_sq%d" % b)
-            nc.scalar.activation(d_sq[:], t1[:], ACT.Square, scale=-0.4, bias=1.0)
             red7 = sbuf([P, PACK, P], F32, "red7_%d" % b)
             neg_sq = sbuf([P, PACK, P], F32, "neg_sq%d" % b)
-            nc.vector.scalar_tensor_tensor(neg_sq[:], t2[:], -0.09, t2[:], ALU.mult, ALU.mult)
             nc.vector.scalar_tensor_tensor(red7[:], shifted[:], 2.5, t2[:], ALU.add, ALU.mult)
+            nc.vector.scalar_tensor_tensor(neg_sq[:], t2[:], -0.5625, t2[:], ALU.mult, ALU.mult)
+            nc.vector.scalar_tensor_tensor(d_sq[:], t1[:], -5.0, t1[:], ALU.add, ALU.mult)
+            red7s.append(red7)
             for t in range(PACK):
                 nc.tensor.transpose(red_bank[t][:, block(b)], red7[:, t, :], ident[:])
             d_sqs.append(d_sq)
             neg_sqs.append(neg_sq)
-            if b == 0:
-                q_banks.append(cross_q(0))
-            picked = sbuf([P, S], F32, "ell_src%d" % b, "shifted%d" % b)
-            for h in range(HALVES):
-                nc.vector.tensor_copy(picked[:, cols(h)], ell_t[:, b, :].indirect(list_half(src_t, h)))
-            ell_src.append(picked)
-        for b in range(1, BLOCKS):
+        for b in range(BLOCKS):
             q_banks.append(cross_q(b))
 
         w3w = sbuf([P, 2 * N], U8, "w3w", "w2w")
         nc.sync.dma_start(w3w[:].bitcast(I32), w3_words[0].bitcast(I32))
         w3s = sbuf([P, 1, N], U8, "w3s", "w2s")
         nc.gpsimd.memset(w3s[:].bitcast(I32), 0)
-        load_scale_rows(nc.sync, w3s, w3_scales)
+        load_scale_rows(nc.sync, w3s, w3_scales, range(QUADS))
 
         den = sbuf([P, PACK, S], F32, "den")
-        num = sbuf([P, PACK, S], F32, "num")
         window = [sbuf([P, S], F32, "window%d" % t) for t in range(PACK)]
         for t in range(PACK):
-            nc.vector.tensor_tensor(den[:, t, :], red_bank[t][:], ell_src[t][:], ALU.mult)
-            nc.vector.scalar_tensor_tensor(num[:, t, :], ell_t[:, t, :], 7.0, red_bank[t][:], ALU.mult, ALU.add)
+            nc.vector.tensor_tensor(den[:, t, :], red_bank[t][:], ell_src[:, t, :], ALU.mult)
 
+        sign = sbuf([P, PACK, S], F32, "sign")
         pulled = sbuf([P, PACK, S], F32, "pulled")
         late_slots = (("t1_3", "d_sq3"), ("t2_3", "ln_q1"))
         for h in range(HALVES):
@@ -184,7 +214,7 @@ def tile_picked_ylensg_log_p_kernel(
             ln_ratio = sbuf([P, PACK, HALF], F32, "ln_ratio%d" % h)
             nc.scalar.activation(ln_flx[:], flx_t[:, :, cols(h)], ACT.Ln)
             for c in range(BLOCKS // HALVES):
-                nc.scalar.activation(ln_q[:, :, block(c)], q_banks[2 * h + c][:], ACT.Ln, bias=0.2)
+                nc.scalar.activation(ln_q[:, :, block(c)], q_banks[2 * h + c][:], ACT.Ln, scale=0.16, bias=1.2)
             if h == 0:
                 for t in range(PACK):
                     nc.scalar.activation(window[t][:], red_bank[t][:], ACT.Copy, scale=u14[:, t : t + 1])
@@ -194,15 +224,18 @@ def tile_picked_ylensg_log_p_kernel(
                     pulled[:, t, cols(h)], window[t][:].indirect(list_half(src_t, h)), ln_ratio[:, t, :], ALU.mult
                 )
 
-        sign = sbuf([P, PACK, S], F32, "sign")
         signed_num = sbuf([P, PACK, S], F32, "signed_num")
         for t in range(PACK):
+            num_bank = bank([P, S], "num_bank%d" % t, q_slot[t])
+            for b in range(BLOCKS):
+                nc.tensor.matmul(num_bank[:, block(b)], ell7[b][:, t, :], ident[:], start=True, stop=False, is_transpose=True)
+                nc.tensor.matmul(num_bank[:, block(b)], red7s[b][:, t, :], ident[:], start=False, stop=True, is_transpose=True)
             nc.scalar.activation(sign[:, t, :], den[:, t, :], ACT.Sign, scale=1.0 / 7.0, bias=1.0)
             nc.vector.scalar_tensor_tensor(
-                signed_num[:, t, :], num[:, t, :], u14[:, t : t + 1], sign[:, t, :], ALU.mult, ALU.mult
+                signed_num[:, t, :], num_bank[:], u14[:, t : t + 1], sign[:, t, :], ALU.mult, ALU.mult
             )
 
-        inv_root = sbuf([P, PACK, S], F32, "inv_root", "xw1")
+        inv_root = sbuf([P, PACK, S], F32, "inv_root", "xw0")
         inv_abs = sbuf([P, PACK, S], F32, "inv_abs")
         obs = sbuf([P, PACK, S], F32, "obs")
         hid = sbuf([P, PACK, S], BF16, "hid")

@@ -26,6 +26,10 @@ BLOCKS = S // P
 HALVES = 2
 HALF = S // HALVES
 LIST_COLS = S // 16
+LINE = 4
+SIGN_ON_VECTOR = 2
+ELL_PLANES_ON_VECTOR = (0, PACK - 1)
+W1_QUADS_ON_SYNC = 1
 
 
 def tile_picked_ylensg_log_p_kernel(
@@ -36,19 +40,13 @@ def tile_picked_ylensg_log_p_kernel(
         held = ctx.enter_context(tc.tile_pool(name="held", bufs=1))
         psum = ctx.enter_context(tc.psum_pool(name="psum", bufs=1))
 
-        def sbuf(shape, dtype, name, slot=None):
-            return held.tile(shape, dtype, name=name, tag=slot or name, align_bytes=64)
+        def sbuf(shape, dtype, name, reuse=None):
+            return held.tile(shape, dtype, name=name, tag=reuse or name, align_bytes=64)
 
         def bank(shape, name, slot):
             return psum.tile(shape, F32, name=name, tag=slot)
 
-        def quad(q):
-            return slice(32 * q, 32 * q + 4)
-
-        def rows(q):
-            return slice(4 * q, 4 * q + 4)
-
-        def cols(h):
+        def half(h):
             return slice(h * HALF, (h + 1) * HALF)
 
         def block(b):
@@ -65,90 +63,88 @@ def tile_picked_ylensg_log_p_kernel(
         w2w = sbuf([P, PASSES, 2 * H], U8, "w2w")
         w1s = sbuf([P, PASSES, H], U8, "w1s")
         w2s = sbuf([P, PASSES, H], U8, "w2s")
-
         ell_t = sbuf([P, PACK, S], F32, "ell_t")
         ident = sbuf([P, P], F32, "ident")
+
         make_identity(nc, ident[:])
         nc.vector.memset(xs[:].bitcast(I32), 0)
         nc.gpsimd.memset(w1s[:].bitcast(I32), 0)
         nc.gpsimd.memset(w2s[:].bitcast(I32), 0)
 
-        def load_scale_rows(engine, plane, scales, quads):
+        def load_scale_rows(engine, scale_tile, scales, quads):
             for q in quads:
                 engine.dma_start(
-                    plane[quad(q), :, :].bitcast(I32), scales[:, rows(q), :].rearrange("o r c -> r o c").bitcast(I32)
+                    scale_tile[32 * q : 32 * q + 4, :, :].bitcast(I32),
+                    scales[:, 4 * q : 4 * q + 4, :].rearrange("o r c -> r o c").bitcast(I32),
                 )
 
-        def load_x_words(o):
-            nc.sync.dma_start(xw[o][:], x_words[o].rearrange("p n r -> p (n r)").bitcast(I32))
-
-        ell_v = ell.rearrange("(p t) j -> p t j", t=PACK)
+        ell_planes = ell.rearrange("(p t) j -> p t j", t=PACK)
         nc.sync.dma_start(src_t[:], src)
-        for pair in range(2):
-            nc.sync.dma_start(ell_t[:, 2 * pair : 2 * pair + 2, :], ell_v[:, 2 * pair : 2 * pair + 2, :])
+        for t in range(0, PACK, 2):
+            nc.sync.dma_start(ell_t[:, t : t + 2, :], ell_planes[:, t : t + 2, :])
         nc.sync.dma_start(offs_t[:], offs)
         load_scale_rows(nc.sync, xs, x_scales, range(QUADS))
-        load_x_words(0)
-        load_x_words(1)
-        load_scale_rows(nc.sync, w1s, w1_scales, range(1))
+        for o in range(PASSES):
+            nc.sync.dma_start(xw[o][:], x_words[o].rearrange("p n r -> p (n r)").bitcast(I32))
+        load_scale_rows(nc.sync, w1s, w1_scales, range(W1_QUADS_ON_SYNC))
         load_scale_rows(nc.sync, w2s, w2_scales, range(QUADS))
         nc.sync.dma_start(w1w[:].bitcast(I32), w1_words.rearrange("o p c -> p o c").bitcast(I32))
         nc.sync.dma_start(w2w[:].bitcast(I32), w2_words.rearrange("o p c -> p o c").bitcast(I32))
-        load_scale_rows(nc.gpsimd, w1s, w1_scales, range(1, QUADS))
+        load_scale_rows(nc.gpsimd, w1s, w1_scales, range(W1_QUADS_ON_SYNC, QUADS))
 
-        ell_src = sbuf([P, PACK, S], F32, "ell_src")
+        ell_src = []
 
-        def gather_ell(t):
+        def look_up_ell(t, reuse=None):
+            picked = sbuf([P, S], F32, "ell_src%d" % t, reuse)
+            ell_src.append(picked)
             for h in range(HALVES):
                 looked_up = ell_t[:, t, :].indirect(list_half(src_t, h))
-                if t in (0, PACK - 1):
-                    nc.vector.tensor_copy(ell_src[:, t, cols(h)], looked_up)
+                if t in ELL_PLANES_ON_VECTOR:
+                    nc.vector.tensor_copy(picked[:, half(h)], looked_up)
                 else:
-                    nc.scalar.activation(ell_src[:, t, cols(h)], looked_up, ACT.Copy)
+                    nc.scalar.activation(picked[:, half(h)], looked_up, ACT.Copy)
 
-        gather_ell(0)
-        gather_ell(1)
+        look_up_ell(0)
+        look_up_ell(1)
+        plane_slots = ["plane%d" % t for t in range(PACK)]
         ell7 = []
         for b in range(BLOCKS):
-            turned = bank([P, PACK, P], "ell_bank%d" % b, "red%d" % b)
+            turned = bank([P, PACK, P], "ell_bank%d" % b, plane_slots[b])
             for t in range(PACK):
                 nc.tensor.transpose(turned[:, t, :], ell_t[:, t, block(b)], ident[:])
             scaled = sbuf([P, PACK, P], F32, "ell7_%d" % b)
             nc.scalar.activation(scaled[:], turned[:], ACT.Copy, scale=7.0)
             ell7.append(scaled)
-        gather_ell(2)
+        look_up_ell(2)
 
-        gw = [sbuf([P, S], U32, "gw%d" % o) for o in range(PASSES)]
-        gs = [sbuf([P, S], U8, "gs%d" % o) for o in range(PASSES)]
-
-        def gather_words(o, h):
-            nc.vector.tensor_copy(gw[o][:, cols(h)], xw[o][:].bitcast(U32).indirect(list_half(offs_t, h)))
-
-        def gather_scales(o, h):
-            nc.vector.tensor_copy(gs[o][:, cols(h)], xs[:, o, :].indirect(list_half(offs_t, h)))
-
+        picked_words = [sbuf([P, S], U32, "picked_words%d" % o) for o in range(PASSES)]
+        picked_scales = [sbuf([P, S], U8, "picked_scales%d" % o) for o in range(PASSES)]
         for h in range(HALVES):
             for o in range(PASSES):
-                gather_scales(o, h)
+                nc.vector.tensor_copy(picked_scales[o][:, half(h)], xs[:, o, :].indirect(list_half(offs_t, h)))
         for o in range(PASSES):
             for h in range(HALVES):
-                gather_words(o, h)
+                nc.vector.tensor_copy(
+                    picked_words[o][:, half(h)], xw[o][:].bitcast(U32).indirect(list_half(offs_t, h))
+                )
 
-        gather_ell(3)
+        look_up_ell(3, "xw1")
         unit_t = sbuf([P, PACK], F32, "unit_t", "xs")
         nc.sync.dma_start(unit_t[:], unit.rearrange("(p t) o -> p (t o)", t=PACK))
         flx_t = sbuf([P, PACK, S], F32, "flx_t", "xw0")
         nc.sync.dma_start(flx_t[:], flx.rearrange("(p t) j -> p t j", t=PACK))
-        u14 = sbuf([P, PACK], F32, "u14")
-        nc.gpsimd.tensor_scalar(u14[:], unit_t[:], 1.0 / 14.0, 0.0, ALU.mult, ALU.add)
+        unit14 = sbuf([P, PACK], F32, "unit14")
+        nc.gpsimd.tensor_scalar(unit14[:], unit_t[:], 1.0 / 14.0, 0.0, ALU.mult, ALU.add)
+        unit7 = sbuf([P, PACK], F32, "unit7")
+        nc.gpsimd.tensor_scalar(unit7[:], unit_t[:], 1.0 / 7.0, 0.0, ALU.mult, ALU.add)
 
         def product(name, slot, words, scales, b):
             acc = bank([P, H], name, slot)
             for o in range(PASSES):
                 nc.tensor.matmul_mx(
                     out=acc[:],
-                    lhsT=gw[o][:, block(b)].bitcast(FP8X4),
-                    lhsT_scale=gs[o][:, block(b)],
+                    lhsT=picked_words[o][:, block(b)].bitcast(FP8X4),
+                    lhsT_scale=picked_scales[o][:, block(b)],
                     rhs=words[:, o, :].bitcast(FP4X4),
                     rhs_scale=scales[:, o, :],
                     start=(o == 0),
@@ -156,43 +152,36 @@ def tile_picked_ylensg_log_p_kernel(
                 )
             return acc[:].rearrange("p (m t) -> p t m", t=PACK)
 
-        ring = ("ring0", "ring1", "ring2", "ring3")
-        red_bank = [bank([P, S], "red_bank%d" % t, "red%d" % t) for t in range(PACK)]
-        q_slot = ring
-        red7s = []
-        d_sqs = []
-        neg_sqs = []
+        def turn_and_add(target, first, second):
+            nc.tensor.matmul(target, first, ident[:], start=True, stop=False, is_transpose=True)
+            nc.tensor.matmul(target, second, ident[:], start=False, stop=True, is_transpose=True)
 
-        def cross_q(b):
-            q_bank = bank([P, PACK, P], "q_bank%d" % b, q_slot[b])
+        ring_slots = ["ring%d" % r for r in range(4)]
+        red_bank = [bank([P, S], "red_bank%d" % t, plane_slots[t]) for t in range(PACK)]
+        red7, kappa_part, shear_part = [], [], []
+        for b in range(BLOCKS):
+            kp = product("kp%d" % b, ring_slots[(2 * b) % 4], w1w, w1s, b)
+            sh = product("sh%d" % b, ring_slots[(2 * b + 1) % 4], w2w, w2s, b)
+            tanh_shifted = sbuf([P, PACK, P], F32, "tanh_shifted%d" % b)
+            tanh_kp = sbuf([P, PACK, P], F32, "tanh_kp%d" % b)
+            tanh_sh = sbuf([P, PACK, P], F32, "tanh_sh%d" % b)
+            nc.scalar.activation(tanh_shifted[:], kp, ACT.Tanh, bias=0.5 * math.log(3.0 / 7.0))
+            nc.scalar.activation(tanh_sh[:], sh, ACT.Tanh)
+            nc.scalar.activation(tanh_kp[:], kp, ACT.Tanh)
+            kappa_part.append(sbuf([P, PACK, P], F32, "kappa_part%d" % b))
+            red7.append(sbuf([P, PACK, P], F32, "red7_%d" % b))
+            shear_part.append(sbuf([P, PACK, P], F32, "shear_part%d" % b))
+            nc.vector.scalar_tensor_tensor(red7[b][:], tanh_shifted[:], 2.5, tanh_sh[:], ALU.add, ALU.mult)
+            nc.vector.scalar_tensor_tensor(shear_part[b][:], tanh_sh[:], -0.5625, tanh_sh[:], ALU.mult, ALU.mult)
+            nc.vector.scalar_tensor_tensor(kappa_part[b][:], tanh_kp[:], -5.0, tanh_kp[:], ALU.add, ALU.mult)
             for t in range(PACK):
-                nc.tensor.matmul(q_bank[:, t, :], d_sqs[b][:, t, :], ident[:], start=True, stop=False, is_transpose=True)
-                nc.tensor.matmul(q_bank[:, t, :], neg_sqs[b][:, t, :], ident[:], start=False, stop=True, is_transpose=True)
-            return q_bank
+                nc.tensor.transpose(red_bank[t][:, block(b)], red7[b][:, t, :], ident[:])
 
-        q_banks = []
+        q_bank = []
         for b in range(BLOCKS):
-            kp = product("kp%d" % b, ring[(2 * b) % 4], w1w, w1s, b)
-            sh = product("sh%d" % b, ring[(2 * b + 1) % 4], w2w, w2s, b)
-            shifted = sbuf([P, PACK, P], F32, "shifted%d" % b)
-            t1 = sbuf([P, PACK, P], F32, "t1_%d" % b)
-            t2 = sbuf([P, PACK, P], F32, "t2_%d" % b)
-            nc.scalar.activation(shifted[:], kp, ACT.Tanh, bias=0.5 * math.log(3.0 / 7.0))
-            nc.scalar.activation(t2[:], sh, ACT.Tanh)
-            nc.scalar.activation(t1[:], kp, ACT.Tanh)
-            d_sq = sbuf([P, PACK, P], F32, "d_sq%d" % b)
-            red7 = sbuf([P, PACK, P], F32, "red7_%d" % b)
-            neg_sq = sbuf([P, PACK, P], F32, "neg_sq%d" % b)
-            nc.vector.scalar_tensor_tensor(red7[:], shifted[:], 2.5, t2[:], ALU.add, ALU.mult)
-            nc.vector.scalar_tensor_tensor(neg_sq[:], t2[:], -0.5625, t2[:], ALU.mult, ALU.mult)
-            nc.vector.scalar_tensor_tensor(d_sq[:], t1[:], -5.0, t1[:], ALU.add, ALU.mult)
-            red7s.append(red7)
+            q_bank.append(bank([P, PACK, P], "q_bank%d" % b, ring_slots[b]))
             for t in range(PACK):
-                nc.tensor.transpose(red_bank[t][:, block(b)], red7[:, t, :], ident[:])
-            d_sqs.append(d_sq)
-            neg_sqs.append(neg_sq)
-        for b in range(BLOCKS):
-            q_banks.append(cross_q(b))
+                turn_and_add(q_bank[b][:, t, :], kappa_part[b][:, t, :], shear_part[b][:, t, :])
 
         w3w = sbuf([P, 2 * N], U8, "w3w", "w2w")
         nc.sync.dma_start(w3w[:].bitcast(I32), w3_words[0].bitcast(I32))
@@ -200,71 +189,79 @@ def tile_picked_ylensg_log_p_kernel(
         nc.gpsimd.memset(w3s[:].bitcast(I32), 0)
         load_scale_rows(nc.sync, w3s, w3_scales, range(QUADS))
 
-        den = sbuf([P, PACK, S], F32, "den")
-        window = [sbuf([P, S], F32, "window%d" % t) for t in range(PACK)]
+        cross = sbuf([P, PACK, S], F32, "cross")
+        red_window = [sbuf([P, S], F32, "red_window%d" % t) for t in range(PACK)]
         for t in range(PACK):
-            nc.vector.tensor_tensor(den[:, t, :], red_bank[t][:], ell_src[:, t, :], ALU.mult)
+            nc.vector.tensor_tensor(cross[:, t, :], red_bank[t][:], ell_src[t][:], ALU.mult)
 
+        last = BLOCKS - 1
+        ln_buffers = (("tanh_kp%d" % last, "tanh_shifted%d" % last), ("tanh_sh%d" % last, None))
         sign = sbuf([P, PACK, S], F32, "sign")
         pulled = sbuf([P, PACK, S], F32, "pulled")
-        late_slots = (("t1_3", "d_sq3"), ("t2_3", "ln_q1"))
         for h in range(HALVES):
-            ln_flx = sbuf([P, PACK, HALF], F32, "ln_flx%d" % h, late_slots[h][0])
-            ln_q = sbuf([P, PACK, HALF], F32, "ln_q%d" % h, late_slots[h][1])
+            ln_flx = sbuf([P, PACK, HALF], F32, "ln_flx%d" % h, ln_buffers[h][0])
+            ln_q = sbuf([P, PACK, HALF], F32, "ln_q%d" % h, ln_buffers[h][1])
             ln_ratio = sbuf([P, PACK, HALF], F32, "ln_ratio%d" % h)
-            nc.scalar.activation(ln_flx[:], flx_t[:, :, cols(h)], ACT.Ln)
+            nc.scalar.activation(ln_flx[:], flx_t[:, :, half(h)], ACT.Ln)
             for c in range(BLOCKS // HALVES):
-                nc.scalar.activation(ln_q[:, :, block(c)], q_banks[2 * h + c][:], ACT.Ln, scale=0.16, bias=1.2)
+                b = h * BLOCKS // HALVES + c
+                nc.scalar.activation(ln_q[:, :, block(c)], q_bank[b][:], ACT.Ln, scale=0.16, bias=1.2)
             if h == 0:
                 for t in range(PACK):
-                    nc.scalar.activation(window[t][:], red_bank[t][:], ACT.Copy, scale=u14[:, t : t + 1])
+                    nc.scalar.activation(red_window[t][:], red_bank[t][:], ACT.Copy, scale=unit14[:, t : t + 1])
             nc.vector.tensor_tensor(ln_ratio[:], ln_q[:], ln_flx[:], ALU.subtract)
             for t in range(PACK):
                 nc.vector.tensor_tensor(
-                    pulled[:, t, cols(h)], window[t][:].indirect(list_half(src_t, h)), ln_ratio[:, t, :], ALU.mult
+                    pulled[:, t, half(h)], red_window[t][:].indirect(list_half(src_t, h)), ln_ratio[:, t, :], ALU.mult
                 )
 
+        nc.vector.tensor_scalar(
+            sign[:, :SIGN_ON_VECTOR, :], cross[:, :SIGN_ON_VECTOR, :], -7.0, 0.5, ALU.is_ge, ALU.subtract
+        )
         signed_num = sbuf([P, PACK, S], F32, "signed_num")
         for t in range(PACK):
-            num_bank = bank([P, S], "num_bank%d" % t, q_slot[t])
+            num_bank = bank([P, S], "num_bank%d" % t, ring_slots[t])
             for b in range(BLOCKS):
-                nc.tensor.matmul(num_bank[:, block(b)], ell7[b][:, t, :], ident[:], start=True, stop=False, is_transpose=True)
-                nc.tensor.matmul(num_bank[:, block(b)], red7s[b][:, t, :], ident[:], start=False, stop=True, is_transpose=True)
-            nc.scalar.activation(sign[:, t, :], den[:, t, :], ACT.Sign, scale=1.0 / 7.0, bias=1.0)
+                turn_and_add(num_bank[:, block(b)], ell7[b][:, t, :], red7[b][:, t, :])
+            if t < SIGN_ON_VECTOR:
+                factor = unit7
+            else:
+                factor = unit14
+                nc.scalar.activation(sign[:, t, :], cross[:, t, :], ACT.Sign, scale=1.0 / 7.0, bias=1.0)
             nc.vector.scalar_tensor_tensor(
-                signed_num[:, t, :], num_bank[:], u14[:, t : t + 1], sign[:, t, :], ALU.mult, ALU.mult
+                signed_num[:, t, :], num_bank[:], factor[:, t : t + 1], sign[:, t, :], ALU.mult, ALU.mult
             )
 
         inv_root = sbuf([P, PACK, S], F32, "inv_root", "xw0")
         inv_abs = sbuf([P, PACK, S], F32, "inv_abs")
         obs = sbuf([P, PACK, S], F32, "obs")
-        hid = sbuf([P, PACK, S], BF16, "hid")
-        out_v = out.rearrange("(g p) j -> p g j", p=P)
-        for c in range(BLOCKS):
+        hid = []
+        out_rows = out.rearrange("(g p) j -> p g j", p=P)
+        for b in range(BLOCKS):
             nc.scalar.activation(
-                inv_root[:, :, block(c)], den[:, :, block(c)], ACT.Abs_reciprocal_sqrt, scale=1.0 / 14.0, bias=0.5
+                inv_root[:, :, block(b)], cross[:, :, block(b)], ACT.Abs_reciprocal_sqrt, scale=1.0 / 14.0, bias=0.5
             )
-            nc.scalar.activation(inv_abs[:, :, block(c)], inv_root[:, :, block(c)], ACT.Square)
+            nc.scalar.activation(inv_abs[:, :, block(b)], inv_root[:, :, block(b)], ACT.Square)
 
-        def observe(c):
-            nc.vector.tensor_tensor(obs[:, :, block(c)], signed_num[:, :, block(c)], inv_abs[:, :, block(c)], ALU.mult)
+        def observe(b):
+            nc.vector.tensor_tensor(obs[:, :, block(b)], signed_num[:, :, block(b)], inv_abs[:, :, block(b)], ALU.mult)
 
-        def combine(c):
-            nc.vector.tensor_tensor(hid[:, :, block(c)], pulled[:, :, block(c)], obs[:, :, block(c)], ALU.add)
+        def combine(b):
+            hid.append(sbuf([P, P, PACK], BF16, "hid%d" % b))
+            nc.vector.tensor_tensor(
+                hid[b][:].rearrange("p (r i) t -> p r t i", i=LINE),
+                pulled[:, :, block(b)].rearrange("p t (r i) -> p r t i", i=LINE),
+                obs[:, :, block(b)].rearrange("p t (r i) -> p r t i", i=LINE),
+                ALU.add,
+            )
 
-        def finish(c):
-            woven = sbuf([P, P, PACK], BF16, "woven%d" % c)
-            planes = hid[:, :, block(c)].rearrange("p t j -> p j t")
-            if c < BLOCKS - 1:
-                nc.scalar.copy(woven[:], planes)
-            else:
-                nc.vector.tensor_copy(woven[:], planes)
-            codes = sbuf([P, P], U32, "codes%d" % c)
-            code_scales = sbuf([P, P], U8, "code_scales%d" % c)
+        def finish(b):
+            codes = sbuf([P, P], U32, "codes%d" % b)
+            code_scales = sbuf([P, P], U8, "code_scales%d" % b)
             nc.vector.quantize_mx(
-                out=codes[:].bitcast(FP8X4), scales=code_scales[:], in_=woven[:].rearrange("p j t -> p (j t)")
+                out=codes[:].bitcast(FP8X4), scales=code_scales[:], in_=hid[b][:].rearrange("p j t -> p (j t)")
             )
-            acc = bank([P, N // P, P], "acc%d" % c, "red%d" % c)
+            acc = bank([P, N // P, P], "acc%d" % b, plane_slots[b])
             for g in range(N // P):
                 nc.tensor.matmul_mx(
                     out=acc[:, g, :],
@@ -275,9 +272,9 @@ def tile_picked_ylensg_log_p_kernel(
                     start=True,
                     stop=True,
                 )
-            result = sbuf([P, N // P, P], F32, "result%d" % c)
+            result = sbuf([P, N // P, P], F32, "result%d" % b)
             nc.scalar.copy(result[:], acc[:])
-            nc.sync.dma_start(out_v[:, :, block(c)], result[:])
+            nc.sync.dma_start(out_rows[:, :, block(b)], result[:])
 
         for step in range(BLOCKS + 2):
             if step < BLOCKS:

import math
from contextlib import ExitStack

import concourse.mybir as mybir
from concourse.masks import make_identity

K, T, S, N, H = 1024, 2048, 512, 256, 512
FLOPS = 2 * (2 * K * H * S + H * N * S)

F32 = mybir.dt.float32
BF16 = mybir.dt.bfloat16
I32 = mybir.dt.int32
U32 = mybir.dt.uint32
U16 = mybir.dt.uint16
U8 = mybir.dt.uint8
FP8X4 = mybir.dt.float8_e4m3fn_x4
FP4X4 = mybir.dt.float4_e2m1fn_x4
ALU = mybir.AluOpType
ACT = mybir.ActivationFunctionType

P = 128
PACK = 4
PASSES = K // (P * PACK)
QUADS = 4
BLOCKS = S // P
HALVES = 2
HALF = S // HALVES
LIST_COLS = S // 16
LINE = 4
SIGN_ON_VECTOR = 2
ELL_PLANES_ON_VECTOR = (0, PACK - 1)
W1_QUADS_ON_SYNC = 1


def tile_picked_ylensg_log_p_kernel(
    tc, x_words, x_scales, w1_words, w1_scales, w2_words, w2_scales, ell, flx, unit, w3_words, w3_scales, offs, src, out
):
    nc = tc.nc
    with ExitStack() as ctx:
        held = ctx.enter_context(tc.tile_pool(name="held", bufs=1))
        psum = ctx.enter_context(tc.psum_pool(name="psum", bufs=1))

        def sbuf(shape, dtype, name, reuse=None):
            return held.tile(shape, dtype, name=name, tag=reuse or name, align_bytes=64)

        def bank(shape, name, slot):
            return psum.tile(shape, F32, name=name, tag=slot)

        def half(h):
            return slice(h * HALF, (h + 1) * HALF)

        def block(b):
            return slice(b * P, (b + 1) * P)

        def list_half(entries, h):
            return entries[:, h * LIST_COLS // HALVES : (h + 1) * LIST_COLS // HALVES]

        offs_t = held.tile([P, LIST_COLS], U16, name="offs_t")
        src_t = held.tile([P, LIST_COLS], U16, name="src_t")
        xw = [sbuf([P, T], I32, "xw%d" % o) for o in range(PASSES)]
        xs = sbuf([P, PASSES, T], U8, "xs")
        w1w = sbuf([P, PASSES, 2 * H], U8, "w1w")
        w2w = sbuf([P, PASSES, 2 * H], U8, "w2w")
        w1s = sbuf([P, PASSES, H], U8, "w1s")
        w2s = sbuf([P, PASSES, H], U8, "w2s")
        ell_t = sbuf([P, PACK, S], F32, "ell_t")
        ident = sbuf([P, P], F32, "ident")

        make_identity(nc, ident[:])
        nc.vector.memset(xs[:].bitcast(I32), 0)
        nc.gpsimd.memset(w1s[:].bitcast(I32), 0)
        nc.gpsimd.memset(w2s[:].bitcast(I32), 0)

        def load_scale_rows(engine, scale_tile, scales, quads):
            for q in quads:
                engine.dma_start(
                    scale_tile[32 * q : 32 * q + 4, :, :].bitcast(I32),
                    scales[:, 4 * q : 4 * q + 4, :].rearrange("o r c -> r o c").bitcast(I32),
                )

        ell_planes = ell.rearrange("(p t) j -> p t j", t=PACK)
        nc.sync.dma_start(src_t[:], src)
        for t in range(0, PACK, 2):
            nc.sync.dma_start(ell_t[:, t : t + 2, :], ell_planes[:, t : t + 2, :])
        nc.sync.dma_start(offs_t[:], offs)
        load_scale_rows(nc.sync, xs, x_scales, range(QUADS))
        for o in range(PASSES):
            nc.sync.dma_start(xw[o][:], x_words[o].rearrange("p n r -> p (n r)").bitcast(I32))
        load_scale_rows(nc.sync, w1s, w1_scales, range(W1_QUADS_ON_SYNC))
        load_scale_rows(nc.sync, w2s, w2_scales, range(QUADS))
        nc.sync.dma_start(w1w[:].bitcast(I32), w1_words.rearrange("o p c -> p o c").bitcast(I32))
        nc.sync.dma_start(w2w[:].bitcast(I32), w2_words.rearrange("o p c -> p o c").bitcast(I32))
        load_scale_rows(nc.gpsimd, w1s, w1_scales, range(W1_QUADS_ON_SYNC, QUADS))

        ell_src = []

        def look_up_ell(t, reuse=None):
            picked = sbuf([P, S], F32, "ell_src%d" % t, reuse)
            ell_src.append(picked)
            for h in range(HALVES):
                looked_up = ell_t[:, t, :].indirect(list_half(src_t, h))
                if t in ELL_PLANES_ON_VECTOR:
                    nc.vector.tensor_copy(picked[:, half(h)], looked_up)
                else:
                    nc.scalar.activation(picked[:, half(h)], looked_up, ACT.Copy)

        look_up_ell(0)
        look_up_ell(1)
        plane_slots = ["plane%d" % t for t in range(PACK)]
        ell7 = []
        for b in range(BLOCKS):
            turned = bank([P, PACK, P], "ell_bank%d" % b, plane_slots[b])
            for t in range(PACK):
                nc.tensor.transpose(turned[:, t, :], ell_t[:, t, block(b)], ident[:])
            scaled = sbuf([P, PACK, P], F32, "ell7_%d" % b)
            nc.scalar.activation(scaled[:], turned[:], ACT.Copy, scale=7.0)
            ell7.append(scaled)
        look_up_ell(2)

        picked_words = [sbuf([P, S], U32, "picked_words%d" % o) for o in range(PASSES)]
        picked_scales = [sbuf([P, S], U8, "picked_scales%d" % o) for o in range(PASSES)]
        for h in range(HALVES):
            for o in range(PASSES):
                nc.vector.tensor_copy(picked_scales[o][:, half(h)], xs[:, o, :].indirect(list_half(offs_t, h)))
        for o in range(PASSES):
            for h in range(HALVES):
                nc.vector.tensor_copy(
                    picked_words[o][:, half(h)], xw[o][:].bitcast(U32).indirect(list_half(offs_t, h))
                )

        look_up_ell(3, "xw1")
        unit_t = sbuf([P, PACK], F32, "unit_t", "xs")
        nc.sync.dma_start(unit_t[:], unit.rearrange("(p t) o -> p (t o)", t=PACK))
        flx_t = sbuf([P, PACK, S], F32, "flx_t", "xw0")
        nc.sync.dma_start(flx_t[:], flx.rearrange("(p t) j -> p t j", t=PACK))
        unit14 = sbuf([P, PACK], F32, "unit14")
        nc.gpsimd.tensor_scalar(unit14[:], unit_t[:], 1.0 / 14.0, 0.0, ALU.mult, ALU.add)
        unit7 = sbuf([P, PACK], F32, "unit7")
        nc.gpsimd.tensor_scalar(unit7[:], unit_t[:], 1.0 / 7.0, 0.0, ALU.mult, ALU.add)

        def product(name, slot, words, scales, b):
            acc = bank([P, H], name, slot)
            for o in range(PASSES):
                nc.tensor.matmul_mx(
                    out=acc[:],
                    lhsT=picked_words[o][:, block(b)].bitcast(FP8X4),
                    lhsT_scale=picked_scales[o][:, block(b)],
                    rhs=words[:, o, :].bitcast(FP4X4),
                    rhs_scale=scales[:, o, :],
                    start=(o == 0),
                    stop=(o == PASSES - 1),
                )
            return acc[:].rearrange("p (m t) -> p t m", t=PACK)

        def turn_and_add(target, first, second):
            nc.tensor.matmul(target, first, ident[:], start=True, stop=False, is_transpose=True)
            nc.tensor.matmul(target, second, ident[:], start=False, stop=True, is_transpose=True)

        ring_slots = ["ring%d" % r for r in range(4)]
        red_bank = [bank([P, S], "red_bank%d" % t, plane_slots[t]) for t in range(PACK)]
        red7, kappa_part, shear_part = [], [], []
        for b in range(BLOCKS):
            kp = product("kp%d" % b, ring_slots[(2 * b) % 4], w1w, w1s, b)
            sh = product("sh%d" % b, ring_slots[(2 * b + 1) % 4], w2w, w2s, b)
            tanh_shifted = sbuf([P, PACK, P], F32, "tanh_shifted%d" % b)
            tanh_kp = sbuf([P, PACK, P], F32, "tanh_kp%d" % b)
            tanh_sh = sbuf([P, PACK, P], F32, "tanh_sh%d" % b)
            nc.scalar.activation(tanh_shifted[:], kp, ACT.Tanh, bias=0.5 * math.log(3.0 / 7.0))
            nc.scalar.activation(tanh_sh[:], sh, ACT.Tanh)
            nc.scalar.activation(tanh_kp[:], kp, ACT.Tanh)
            kappa_part.append(sbuf([P, PACK, P], F32, "kappa_part%d" % b))
            red7.append(sbuf([P, PACK, P], F32, "red7_%d" % b))
            shear_part.append(sbuf([P, PACK, P], F32, "shear_part%d" % b))
            nc.vector.scalar_tensor_tensor(red7[b][:], tanh_shifted[:], 2.5, tanh_sh[:], ALU.add, ALU.mult)
            nc.vector.scalar_tensor_tensor(shear_part[b][:], tanh_sh[:], -0.5625, tanh_sh[:], ALU.mult, ALU.mult)
            nc.vector.scalar_tensor_tensor(kappa_part[b][:], tanh_kp[:], -5.0, tanh_kp[:], ALU.add, ALU.mult)
            for t in range(PACK):
                nc.tensor.transpose(red_bank[t][:, block(b)], red7[b][:, t, :], ident[:])

        q_bank = []
        for b in range(BLOCKS):
            q_bank.append(bank([P, PACK, P], "q_bank%d" % b, ring_slots[b]))
            for t in range(PACK):
                turn_and_add(q_bank[b][:, t, :], kappa_part[b][:, t, :], shear_part[b][:, t, :])

        w3w = sbuf([P, 2 * N], U8, "w3w", "w2w")
        nc.sync.dma_start(w3w[:].bitcast(I32), w3_words[0].bitcast(I32))
        w3s = sbuf([P, 1, N], U8, "w3s", "w2s")
        nc.gpsimd.memset(w3s[:].bitcast(I32), 0)
        load_scale_rows(nc.sync, w3s, w3_scales, range(QUADS))

        cross = sbuf([P, PACK, S], F32, "cross")
        red_window = [sbuf([P, S], F32, "red_window%d" % t) for t in range(PACK)]
        for t in range(PACK):
            nc.vector.tensor_tensor(cross[:, t, :], red_bank[t][:], ell_src[t][:], ALU.mult)

        last = BLOCKS - 1
        ln_buffers = (("tanh_kp%d" % last, "tanh_shifted%d" % last), ("tanh_sh%d" % last, None))
        sign = sbuf([P, PACK, S], F32, "sign")
        pulled = sbuf([P, PACK, S], F32, "pulled")
        for h in range(HALVES):
            ln_flx = sbuf([P, PACK, HALF], F32, "ln_flx%d" % h, ln_buffers[h][0])
            ln_q = sbuf([P, PACK, HALF], F32, "ln_q%d" % h, ln_buffers[h][1])
            ln_ratio = sbuf([P, PACK, HALF], F32, "ln_ratio%d" % h)
            nc.scalar.activation(ln_flx[:], flx_t[:, :, half(h)], ACT.Ln)
            for c in range(BLOCKS // HALVES):
                b = h * BLOCKS // HALVES + c
                nc.scalar.activation(ln_q[:, :, block(c)], q_bank[b][:], ACT.Ln, scale=0.16, bias=1.2)
            if h == 0:
                for t in range(PACK):
                    nc.scalar.activation(red_window[t][:], red_bank[t][:], ACT.Copy, scale=unit14[:, t : t + 1])
            nc.vector.tensor_tensor(ln_ratio[:], ln_q[:], ln_flx[:], ALU.subtract)
            for t in range(PACK):
                nc.vector.tensor_tensor(
                    pulled[:, t, half(h)], red_window[t][:].indirect(list_half(src_t, h)), ln_ratio[:, t, :], ALU.mult
                )

        nc.vector.tensor_scalar(
            sign[:, :SIGN_ON_VECTOR, :], cross[:, :SIGN_ON_VECTOR, :], -7.0, 0.5, ALU.is_ge, ALU.subtract
        )
        signed_num = sbuf([P, PACK, S], F32, "signed_num")
        for t in range(PACK):
            num_bank = bank([P, S], "num_bank%d" % t, ring_slots[t])
            for b in range(BLOCKS):
                turn_and_add(num_bank[:, block(b)], ell7[b][:, t, :], red7[b][:, t, :])
            if t < SIGN_ON_VECTOR:
                factor = unit7
            else:
                factor = unit14
                nc.scalar.activation(sign[:, t, :], cross[:, t, :], ACT.Sign, scale=1.0 / 7.0, bias=1.0)
            nc.vector.scalar_tensor_tensor(
                signed_num[:, t, :], num_bank[:], factor[:, t : t + 1], sign[:, t, :], ALU.mult, ALU.mult
            )

        inv_root = sbuf([P, PACK, S], F32, "inv_root", "xw0")
        inv_abs = sbuf([P, PACK, S], F32, "inv_abs")
        obs = sbuf([P, PACK, S], F32, "obs")
        hid = []
        out_rows = out.rearrange("(g p) j -> p g j", p=P)
        for b in range(BLOCKS):
            nc.scalar.activation(
                inv_root[:, :, block(b)], cross[:, :, block(b)], ACT.Abs_reciprocal_sqrt, scale=1.0 / 14.0, bias=0.5
            )
            nc.scalar.activation(inv_abs[:, :, block(b)], inv_root[:, :, block(b)], ACT.Square)

        def observe(b):
            nc.vector.tensor_tensor(obs[:, :, block(b)], signed_num[:, :, block(b)], inv_abs[:, :, block(b)], ALU.mult)

        def combine(b):
            hid.append(sbuf([P, P, PACK], BF16, "hid%d" % b))
            nc.vector.tensor_tensor(
                hid[b][:].rearrange("p (r i) t -> p r t i", i=LINE),
                pulled[:, :, block(b)].rearrange("p t (r i) -> p r t i", i=LINE),
                obs[:, :, block(b)].rearrange("p t (r i) -> p r t i", i=LINE),
                ALU.add,
            )

        def finish(b):
            codes = sbuf([P, P], U32, "codes%d" % b)
            code_scales = sbuf([P, P], U8, "code_scales%d" % b)
            nc.vector.quantize_mx(
                out=codes[:].bitcast(FP8X4), scales=code_scales[:], in_=hid[b][:].rearrange("p j t -> p (j t)")
            )
            acc = bank([P, N // P, P], "acc%d" % b, plane_slots[b])
            for g in range(N // P):
                nc.tensor.matmul_mx(
                    out=acc[:, g, :],
                    lhsT=w3w[:, 2 * P * g : 2 * P * (g + 1)].bitcast(FP4X4),
                    lhsT_scale=w3s[:, 0, block(g)],
                    rhs=codes[:].bitcast(FP8X4),
                    rhs_scale=code_scales[:],
                    start=True,
                    stop=True,
                )
            result = sbuf([P, N // P, P], F32, "result%d" % b)
            nc.scalar.copy(result[:], acc[:])
            nc.sync.dma_start(out_rows[:, :, block(b)], result[:])

        for step in range(BLOCKS + 2):
            if step < BLOCKS:
                observe(step)
            if 1 <= step <= BLOCKS:
                combine(step - 1)
            if step >= 2:
                finish(step - 2)
